import numpy as np
import ml_dtypes


def mxq(x, axis, fmt="e4m3"):
    dtype, down = {"e4m3": (ml_dtypes.float8_e4m3fn, 7), "e5m2": (ml_dtypes.float8_e5m2, 14)}[fmt]
    v = np.moveaxis(np.asarray(x, np.float32).astype(ml_dtypes.bfloat16).astype(np.float64), axis, -1)
    blocks = v.reshape(v.shape[:-1] + (-1, 32))
    amax = np.abs(blocks).max(-1, keepdims=True)
    byte = np.maximum(np.where(amax > 0, np.frexp(amax)[1] - 1 + 127, 0) - down, 1)
    scale = np.exp2(byte - 127.0)
    codes = (blocks / scale).astype(np.float32).astype(dtype).astype(np.float64)
    return np.moveaxis((codes * scale).reshape(v.shape), -1, axis)


WIDE = False


def mx_kscale(k):
    if not WIDE:
        return np.ones(k)
    levels = np.array([24, -24, 12, -12, 0])
    if k % 512:
        return np.exp2(np.random.permutation(np.resize(levels, k // 32))).repeat(32)
    a = np.empty((k // 512, 16))
    for p in range(k // 512):
        a[p, :8] = np.random.permutation(np.resize(levels, 8))
        for g in range(8):
            far = levels[np.abs(levels - a[p, g]) >= 10]
            a[p, g + 8] = far[np.random.randint(len(far))]
    return np.exp2(a.ravel()).repeat(32)


def f64(x):
    return np.asarray(x).astype(np.float64)


def striped(idx):
    return np.tile(idx.reshape(-1, 16).T, (8, 1)).astype(np.uint16)


def unstriped(offs):
    return offs[:16].T.reshape(-1).astype(np.int64)


E2M1 = np.array([0.0, 0.5, 1.0, 1.5, 2.0, 3.0, 4.0, 6.0, -0.0, -0.5, -1.0, -1.5, -2.0, -3.0, -4.0, -6.0])


def pack_weight(w, fmt):
    k, n = w.shape
    w = f64(np.asarray(w, np.float32).astype(ml_dtypes.bfloat16)).reshape(k // 32, 32, n)
    amax = np.abs(w).max(1)
    if fmt == "e4m3":
        byte = np.frexp(amax)[1] - 1 + 127 - 7
    else:
        mant, ex = np.frexp(amax / 6.0)
        byte = np.where(mant > 0.5, ex, ex - 1) + 127
    byte = np.clip(np.where(amax > 0, byte, 1), 1, 254)
    scaled = (w * np.exp2(127.0 - byte)[:, None, :]).reshape(k, n).astype(np.float32)
    by_word = np.ascontiguousarray(scaled.reshape(k // 512, 128, 4, n).transpose(0, 1, 3, 2))
    if fmt == "e4m3":
        words = by_word.astype(ml_dtypes.float8_e4m3fn).view(np.uint8)
    else:
        c = by_word.astype(ml_dtypes.float4_e2m1fn).view(np.uint8) & 0xF
        words = (c[..., 0::2] | (c[..., 1::2] << 4)).reshape(k // 512, 128, 2 * n)
    return np.ascontiguousarray(words), np.ascontiguousarray(byte.astype(np.uint8).reshape(k // 512, 16, n))


def unpack_weight(words, scales, fmt):
    g, _, n = scales.shape
    words = np.ascontiguousarray(words).reshape(g, 128, n, -1)
    if fmt == "e4m3":
        vals = words.view(ml_dtypes.float8_e4m3fn).astype(np.float64)
    else:
        nib = np.empty((g, 128, n, 4), np.uint8)
        nib[..., 0::2] = words & 0xF
        nib[..., 1::2] = words >> 4
        vals = E2M1[nib]
    vals = vals * np.repeat(np.exp2(scales.astype(np.float64) - 127.0), 8, axis=1)[..., None]
    return vals.transpose(0, 1, 3, 2).reshape(g * 512, n)


def planes(y):
    n, m = y.shape
    v = y.astype(np.float32).astype(ml_dtypes.bfloat16).astype(np.float64).reshape(n // 32, 32, m)
    top = np.abs(v).max(1)
    byte = np.clip(np.where(top > 0, np.frexp(top)[1] - 1 + 127 - 7, 1), 1, 254)
    codes = (v * np.exp2(127.0 - byte)[:, None, :]).reshape(n, m).astype(np.float32).astype(ml_dtypes.float8_e4m3fn).view(np.uint8)
    words = codes.reshape(n // 512, 128, 4, m).transpose(0, 1, 3, 2)
    return np.ascontiguousarray(words), np.ascontiguousarray(byte.astype(np.uint8).reshape(n // 512, 16, m))


def sigm(f):
    return 1.0 / (1.0 + np.exp(-np.maximum(f, -700.0)))


K, N, T, J = 1024, 512, 2048, 1024


def setup_inputs():
    n = np.random.standard_normal
    s = mx_kscale(K)[:, None]
    p_tab = pack_weight(n((K, T)) * s, "e4m3")
    p_wb = pack_weight(n((K, N)) / np.sqrt(2 * K) / s, "e4m3")
    p_wc = pack_weight(n((K, N)) / np.sqrt(K) / s, "e4m3")
    return {
        "tab_words": p_tab[0],
        "tab_scales": p_tab[1],
        "wa": (n((K, N)) / np.sqrt(2 * K) / s).astype(np.float32),
        "wb_words": p_wb[0],
        "wb_scales": p_wb[1],
        "wc_words": p_wc[0],
        "wc_scales": p_wc[1],
        "rT": (n((N, T))).astype(np.float32),
        "wgo": np.tile(np.random.uniform(0.5, 2.0, J), (128, 1)).astype(np.float32),
        "offs": striped(np.random.permutation(T)[:J]),
        "offs2": striped(np.random.permutation(T)[:J]),
    }


def reference(tab_words, tab_scales, wa, wb_words, wb_scales, wc_words, wc_scales, rT, wgo, offs, offs2):
    idx = unstriped(offs)
    idx2 = unstriped(offs2)
    tab_ = unpack_weight(tab_words, tab_scales, "e4m3")[:, idx]
    tabb_ = unpack_weight(tab_words, tab_scales, "e4m3")[:, idx2]
    wa_ = mxq(f64(wa), 0, "e4m3")
    wb_ = unpack_weight(wb_words, wb_scales, "e4m3")
    za = wa_.T @ tabb_ + wb_.T @ tab_
    eta = sigm(za)
    wc_ = unpack_weight(wc_words, wc_scales, "e4m3")
    ms = wc_.T @ tab_
    out = np.zeros((N, T))
    out[:, idx2] = f64(wgo)[0] * (eta * ms + f64(rT)[:, idx2])
    return (out,) + planes(out)

@@ -1,0 +1,210 @@
+from contextlib import ExitStack
+
+import concourse.mybir as mybir
+
+K, N, T, J = 1024, 512, 2048, 1024
+FLOPS = 2 * 3 * K * N * J
+
+F32 = mybir.dt.float32
+BF16 = mybir.dt.bfloat16
+I32 = mybir.dt.int32
+U32 = mybir.dt.uint32
+U16 = mybir.dt.uint16
+U8 = mybir.dt.uint8
+FP8X4 = mybir.dt.float8_e4m3fn_x4
+ALU = mybir.AluOpType
+ACT = mybir.ActivationFunctionType
+
+P = 128
+PACK = 4
+PASSES = 2
+HALF = 512
+PAGE_ORDER = (2, 0, 1, 3)
+VECTOR_PRODUCT = ()
+CHUNKS = ((0, 512), (512, 384), (896, 384), (1280, 384), (1664, 384))
+VECTOR_CHUNKS = 2
+STORE_GROUPS = ((0, 1), (2, 3), (4,))
+
+
+def tile_list_rgg_LP_kernel(
+    tc, tab_words, tab_scales, wa, wb_words, wb_scales, wc_words, wc_scales, rT, wgo, offs, offs2,
+    out_0, out_1, out_2,
+):
+    nc = tc.nc
+    with ExitStack() as ctx:
+        keep = ctx.enter_context(tc.tile_pool(name="keep", bufs=1))
+        ring = ctx.enter_context(tc.tile_pool(name="ring", bufs=6))
+        psum = ctx.enter_context(tc.psum_pool(name="psum", bufs=4))
+
+        src_list = keep.tile([P, J // 16], U16, name="src_list")
+        dst_list = keep.tile([P, J // 16], U16, name="dst_list")
+        tab_w = [keep.tile([P, T], U32, name="tab_w%d" % a, align_bytes=64) for a in range(PASSES)]
+        tab_s = keep.tile([P, T], U8, name="tab_s", align_bytes=64)
+        w_s_raw = keep.tile([P, N], U8, name="w_s_raw", align_bytes=64)
+        pages = [keep.tile([P, T], F32, name="page%d" % t, align_bytes=64) for t in range(PACK)]
+
+        nc.gpsimd.memset(tab_s[:].bitcast(I32), 0)
+        nc.gpsimd.memset(w_s_raw[:].bitcast(I32), 0)
+        for t in PAGE_ORDER:
+            nc.gpsimd.memset(pages[t][:], 0.0)
+
+        def load_tab_words(a):
+            nc.sync.dma_start(out=tab_w[a][:].bitcast(I32), in_=tab_words[a].rearrange("p t i -> p (t i)").bitcast(I32))
+
+        def load_scale_rows(tile, first_row, scales):
+            for q in range(4):
+                nc.sync.dma_start(
+                    out=tile[32 * q + first_row : 32 * q + first_row + 8, :].bitcast(I32),
+                    in_=scales[:, 4 * q : 4 * q + 4, :].bitcast(I32),
+                )
+
+        nc.sync.dma_start(src_list[:], offs)
+        load_scale_rows(tab_s, 8, tab_scales)
+        load_tab_words(0)
+        nc.sync.dma_start(dst_list[:], offs2)
+        load_tab_words(1)
+
+        def load_weight_scale_rows(q):
+            for first_row, scales in ((0, wb_scales), (8, wc_scales)):
+                nc.sync.dma_start(
+                    out=w_s_raw[32 * q + first_row : 32 * q + first_row + 8, :].bitcast(I32),
+                    in_=scales[:, 4 * q : 4 * q + 4, :].bitcast(I32),
+                )
+
+        wa_raw = []
+        for a in range(PASSES):
+            load_weight_scale_rows(a)
+            raw = keep.tile([P, PACK, N], F32, name="wa_raw%d" % a, align_bytes=64)
+            nc.sync.dma_start(out=raw[:], in_=wa[512 * a : 512 * (a + 1), :].rearrange("(p i) n -> p i n", i=PACK))
+            wa_raw.append(raw)
+        w_raw = []
+        for pos, words in enumerate((wc_words, wb_words)):
+            load_weight_scale_rows(PASSES + pos)
+            raw = keep.tile([P, PASSES, N], U32, name="w_raw%d" % pos, align_bytes=64)
+            nc.sync.dma_start(out=raw[:].bitcast(I32), in_=words.rearrange("a p n i -> p a (n i)").bitcast(I32))
+            w_raw.append(raw)
+        r_rows = rT.rearrange("(p t) c -> p t c", t=PACK)
+        r_pages = {}
+        wgo_sb = keep.tile([P, J], F32, name="wgo_sb", align_bytes=64)
+        for pos, t in enumerate(PAGE_ORDER):
+            r_pages[t] = keep.tile([P, T], F32, name="r_page%d" % t, align_bytes=64)
+            nc.sync.dma_start(out=r_pages[t][:], in_=r_rows[:, t, :])
+            if pos == 0:
+                nc.sync.dma_start(out=wgo_sb[:], in_=wgo)
+
+        def half_of(lst, h):
+            return lst[:, 32 * h : 32 * (h + 1)]
+
+        g_w = {}
+        g_s = {}
+        for h in range(2):
+            for which, lst in enumerate((src_list, dst_list)):
+                g_s[which, h] = keep.tile([P, HALF], U8, name="g_s%d%d" % (which, h), align_bytes=64)
+                nc.vector.tensor_copy(out=g_s[which, h][:], in_=tab_s[:].indirect(half_of(lst, h)))
+        for a in range(PASSES):
+            for h in range(2):
+                for which, lst in enumerate((src_list, dst_list)):
+                    g_w[which, a, h] = keep.tile([P, HALF], U32, name="g_w%d%d%d" % (which, a, h), align_bytes=64)
+                    nc.vector.tensor_copy(out=g_w[which, a, h][:], in_=tab_w[a][:].indirect(half_of(lst, h)))
+
+        wa_w = []
+        wa_s = []
+        for a in range(PASSES):
+            grouped = keep.tile([P, N * PACK], BF16, name="wa_grouped%d" % a, align_bytes=64)
+            nc.scalar.copy(
+                out=grouped[:].rearrange("p (t m i) -> p m t i", t=PACK, i=PACK),
+                in_=wa_raw[a][:].rearrange("p i (m t) -> p m t i", t=PACK),
+            )
+            codes = keep.tile([P, N], U32, name="wa_w%d" % a, align_bytes=64)
+            plane = keep.tile([P, N], U8, name="wa_s%d" % a, align_bytes=64)
+            nc.vector.quantize_mx(out=codes[:].bitcast(FP8X4), scales=plane[:], in_=grouped[:])
+            wa_w.append(codes)
+            wa_s.append(plane)
+
+        w_dealt = []
+        for pos, raw in enumerate(w_raw):
+            per_pass = []
+            for a in range(PASSES):
+                dealt = keep.tile([P, N], U32, name="w_dealt%d%d" % (pos, a), align_bytes=64)
+                nc.scalar.copy(
+                    out=dealt[:].rearrange("p (t u v) -> p u t v", t=PACK, v=4),
+                    in_=raw[:, a, :].rearrange("p (u v t) -> p u t v", t=PACK, v=4),
+                )
+                per_pass.append(dealt)
+            w_dealt.append(per_pass)
+        wc_w, wb_w = w_dealt
+        w_s = keep.tile([P, N], U8, name="w_s", align_bytes=64)
+        nc.gpsimd.tensor_copy(
+            out=w_s[:].rearrange("p (t u v) -> p u t v", t=PACK, v=16),
+            in_=w_s_raw[:].rearrange("p (u v t) -> p u t v", t=PACK, v=16),
+        )
+
+        r_g = {}
+        for t in PAGE_ORDER:
+            for h in range(2):
+                r_g[t, h] = keep.tile([P, HALF], F32, name="r_g%d%d" % (t, h), align_bytes=64)
+                nc.vector.tensor_copy(out=r_g[t, h][:], in_=r_pages[t][:].indirect(half_of(dst_list, h)))
+
+        def mx(acc, w, w_plane, w_row, t, which, a, h, start, stop):
+            cols = slice(P * t, P * (t + 1))
+            nc.tensor.matmul_mx(
+                out=acc[:],
+                lhsT=w[:, cols].bitcast(FP8X4),
+                lhsT_scale=w_plane[w_row:P, cols],
+                rhs=g_w[which, a, h][:].bitcast(FP8X4),
+                rhs_scale=g_s[which, h][8 + 4 * a : P, :],
+                start=start,
+                stop=stop,
+            )
+
+        inter = [keep.tile([P, w, PACK], BF16, name="inter%d" % c, align_bytes=64) for c, (c0, w) in enumerate(CHUNKS)]
+        out_rows = out_0.rearrange("(p t) c -> p t c", t=PACK)
+        unit = 0
+        for pos, t in enumerate(PAGE_ORDER):
+            for h in range(2):
+                ms_ps = psum.tile([P, HALF], F32, name="ms_ps")
+                for a in range(PASSES):
+                    mx(ms_ps, wc_w[a], w_s, 8 + 4 * a, t, 0, a, h, a == 0, a == PASSES - 1)
+                za_ps = psum.tile([P, HALF], F32, name="za_ps")
+                for a in range(PASSES):
+                    mx(za_ps, wb_w[a], w_s, 4 * a, t, 0, a, h, a == 0, False)
+                for a in range(PASSES):
+                    mx(za_ps, wa_w[a], wa_s[a], 0, t, 1, a, h, False, a == PASSES - 1)
+                val = ring.tile([P, HALF], F32, name="val")
+                if unit in VECTOR_PRODUCT:
+                    nc.scalar.activation(out=val[:], in_=za_ps[:], func=ACT.Sigmoid)
+                    nc.vector.tensor_tensor(out=val[:], in0=ms_ps[:], in1=val[:], op=ALU.mult)
+                else:
+                    ms_sb = ring.tile([P, HALF], F32, name="ms_sb")
+                    nc.scalar.copy(out=ms_sb[:], in_=ms_ps[:])
+                    nc.scalar.activation(out=val[:], in_=za_ps[:], func=ACT.Sigmoid)
+                    nc.gpsimd.tensor_tensor(out=val[:], in0=val[:], in1=ms_sb[:], op=ALU.mult)
+                nc.gpsimd.tensor_tensor(out=val[:], in0=val[:], in1=r_g[t, h][:], op=ALU.add)
+                nc.gpsimd.tensor_tensor(out=val[:], in0=val[:], in1=wgo_sb[:, HALF * h : HALF * (h + 1)], op=ALU.mult)
+                nc.vector.tensor_copy(out=pages[t][:].indirect(half_of(dst_list, h)), in_=val[:])
+                unit = unit + 1
+            nc.sync.dma_start(out=out_rows[:, t, :], in_=pages[t][:])
+            for c, (c0, w) in enumerate(CHUNKS):
+                if pos == PACK - 1 and c < VECTOR_CHUNKS:
+                    nc.vector.tensor_copy(out=inter[c][:, :, t], in_=pages[t][:, c0 : c0 + w])
+                else:
+                    nc.scalar.copy(out=inter[c][:, :, t], in_=pages[t][:, c0 : c0 + w])
+
+        out_s = keep.tile([P, T], U8, name="out_s", align_bytes=64)
+        out_words = out_1[0].rearrange("p t i -> p (t i)").bitcast(I32)
+        for g, group in enumerate(STORE_GROUPS):
+            g0 = CHUNKS[group[0]][0]
+            width = sum(CHUNKS[c][1] for c in group)
+            codes = keep.tile([P, width], U32, name="out_w%d" % g, align_bytes=64)
+            for c in group:
+                c0, w = CHUNKS[c]
+                nc.vector.quantize_mx(
+                    out=codes[:, c0 - g0 : c0 - g0 + w].bitcast(FP8X4),
+                    scales=out_s[:, c0 : c0 + w],
+                    in_=inter[c][:].rearrange("p c i -> p (c i)"),
+                )
+            nc.sync.dma_start(out=out_words[:, g0 : g0 + width], in_=codes[:].bitcast(I32))
+        for q in range(4):
+            nc.sync.dma_start(
+                out=out_2[0, 4 * q : 4 * q + 4, :].bitcast(I32), in_=out_s[32 * q : 32 * q + 4, :].bitcast(I32)
+            )

@@ -1,6 +1,7 @@
 from contextlib import ExitStack
 
 import concourse.mybir as mybir
+from concourse.masks import make_identity
 
 K, N, T, J = 1024, 512, 2048, 1024
 FLOPS = 2 * 3 * K * N * J
@@ -19,10 +20,13 @@ P = 128
 PACK = 4
 PASSES = 2
 HALF = 512
+BLOCKS = HALF // P
+SRC, DST = 0, 1
 PAGE_ORDER = (2, 0, 1, 3)
-VECTOR_PRODUCT = ()
+HALF_ORDER = ((0, 0), (1, 0), (0, 1), (1, 1), (2, 0), (2, 1), (3, 0), (3, 1))
 CHUNKS = ((0, 512), (512, 384), (896, 384), (1280, 384), (1664, 384))
 VECTOR_CHUNKS = 2
+GPSIMD_CHUNKS = (2, 3, 4,)
 STORE_GROUPS = ((0, 1), (2, 3), (4,))
 
 
@@ -33,162 +37,235 @@ def tile_list_rgg_LP_kernel(
     nc = tc.nc
     with ExitStack() as ctx:
         keep = ctx.enter_context(tc.tile_pool(name="keep", bufs=1))
-        ring = ctx.enter_context(tc.tile_pool(name="ring", bufs=6))
-        psum = ctx.enter_context(tc.psum_pool(name="psum", bufs=4))
+        ring = ctx.enter_context(tc.tile_pool(name="ring", bufs=8))
+        psum = ctx.enter_context(tc.psum_pool(name="psum", bufs=1))
 
         src_list = keep.tile([P, J // 16], U16, name="src_list")
         dst_list = keep.tile([P, J // 16], U16, name="dst_list")
         tab_w = [keep.tile([P, T], U32, name="tab_w%d" % a, align_bytes=64) for a in range(PASSES)]
         tab_s = keep.tile([P, T], U8, name="tab_s", align_bytes=64)
-        w_s_raw = keep.tile([P, N], U8, name="w_s_raw", align_bytes=64)
+        w_s = keep.tile([P, N], U8, name="w_s", align_bytes=64)
+        wb_w = keep.tile([P, PASSES, N], U32, name="wb_w", align_bytes=64)
+        wc_w = keep.tile([P, PASSES, N], U32, name="wc_w", align_bytes=64)
+        wa_raw = {}
+        for a in range(PASSES):
+            for s in range(2):
+                wa_raw[a, s] = keep.tile([P, PACK, N // 2], F32, name="wa_raw%d%d" % (a, s), tag="wa_raw%d%d" % (a, s), align_bytes=64)
+        wgo_rows = keep.tile([P, P], F32, name="wgo_rows", align_bytes=64)
+        r_pages = [keep.tile([P, T], F32, name="r_page%d" % t, align_bytes=64) for t in range(PACK)]
         pages = [keep.tile([P, T], F32, name="page%d" % t, align_bytes=64) for t in range(PACK)]
+        ident = keep.tile([P, P], F32, name="ident", align_bytes=64)
 
-        nc.gpsimd.memset(tab_s[:].bitcast(I32), 0)
-        nc.gpsimd.memset(w_s_raw[:].bitcast(I32), 0)
+        nc.vector.memset(tab_s[:].bitcast(I32), 0)
+        nc.vector.memset(w_s[:].bitcast(I32), 0)
+        make_identity(nc, ident[:])
         for t in PAGE_ORDER:
             nc.gpsimd.memset(pages[t][:], 0.0)
 
-        def load_tab_words(a):
+        def load_table_words(a):
             nc.sync.dma_start(out=tab_w[a][:].bitcast(I32), in_=tab_words[a].rearrange("p t i -> p (t i)").bitcast(I32))
 
-        def load_scale_rows(tile, first_row, scales):
-            for q in range(4):
-                nc.sync.dma_start(
-                    out=tile[32 * q + first_row : 32 * q + first_row + 8, :].bitcast(I32),
-                    in_=scales[:, 4 * q : 4 * q + 4, :].bitcast(I32),
-                )
+        def load_weight_words(tile, words):
+            nc.sync.dma_start(out=tile[:].bitcast(I32), in_=words.rearrange("a p n i -> p a (n i)").bitcast(I32))
 
-        nc.sync.dma_start(src_list[:], offs)
-        load_scale_rows(tab_s, 8, tab_scales)
-        load_tab_words(0)
-        nc.sync.dma_start(dst_list[:], offs2)
-        load_tab_words(1)
+        def load_scale_rows(tile, first_row, scales, q):
+            nc.sync.dma_start(
+                out=tile[32 * q + first_row : 32 * q + first_row + 8, :].bitcast(I32),
+                in_=scales[:, 4 * q : 4 * q + 4, :].bitcast(I32),
+            )
 
-        def load_weight_scale_rows(q):
-            for first_row, scales in ((0, wb_scales), (8, wc_scales)):
-                nc.sync.dma_start(
-                    out=w_s_raw[32 * q + first_row : 32 * q + first_row + 8, :].bitcast(I32),
-                    in_=scales[:, 4 * q : 4 * q + 4, :].bitcast(I32),
-                )
+        def load_wa(a):
+            rows = wa[512 * a : 512 * (a + 1), :].rearrange("(p i) n -> p i n", i=PACK)
+            for s in range(2):
+                nc.sync.dma_start(out=wa_raw[a, s][:], in_=rows[:, :, N // 2 * s : N // 2 * (s + 1)])
 
-        wa_raw = []
-        for a in range(PASSES):
-            load_weight_scale_rows(a)
-            raw = keep.tile([P, PACK, N], F32, name="wa_raw%d" % a, align_bytes=64)
-            nc.sync.dma_start(out=raw[:], in_=wa[512 * a : 512 * (a + 1), :].rearrange("(p i) n -> p i n", i=PACK))
-            wa_raw.append(raw)
-        w_raw = []
-        for pos, words in enumerate((wc_words, wb_words)):
-            load_weight_scale_rows(PASSES + pos)
-            raw = keep.tile([P, PASSES, N], U32, name="w_raw%d" % pos, align_bytes=64)
-            nc.sync.dma_start(out=raw[:].bitcast(I32), in_=words.rearrange("a p n i -> p a (n i)").bitcast(I32))
-            w_raw.append(raw)
         r_rows = rT.rearrange("(p t) c -> p t c", t=PACK)
-        r_pages = {}
-        wgo_sb = keep.tile([P, J], F32, name="wgo_sb", align_bytes=64)
-        for pos, t in enumerate(PAGE_ORDER):
-            r_pages[t] = keep.tile([P, T], F32, name="r_page%d" % t, align_bytes=64)
+        nc.sync.dma_start(src_list[:], offs)
+        load_weight_words(wc_w, wc_words)
+        load_scale_rows(tab_s, 0, tab_scales, 0)
+        load_scale_rows(tab_s, 0, tab_scales, 1)
+        load_scale_rows(tab_s, 0, tab_scales, 2)
+        load_scale_rows(tab_s, 0, tab_scales, 3)
+        nc.sync.dma_start(dst_list[:], offs2)
+        load_table_words(0)
+        load_table_words(1)
+        load_scale_rows(w_s, 8, wc_scales, 0)
+        load_scale_rows(w_s, 0, wb_scales, 0)
+        load_scale_rows(w_s, 8, wc_scales, 1)
+        load_scale_rows(w_s, 0, wb_scales, 1)
+        nc.sync.dma_start(out=wgo_rows[:], in_=wgo[0:16, :].rearrange("r (b j) -> (r b) j", j=P))
+        load_wa(0)
+        load_scale_rows(w_s, 8, wc_scales, 2)
+        load_scale_rows(w_s, 0, wb_scales, 2)
+        load_scale_rows(w_s, 8, wc_scales, 3)
+        load_scale_rows(w_s, 0, wb_scales, 3)
+        load_wa(1)
+        load_weight_words(wb_w, wb_words)
+        for t in PAGE_ORDER:
             nc.sync.dma_start(out=r_pages[t][:], in_=r_rows[:, t, :])
-            if pos == 0:
-                nc.sync.dma_start(out=wgo_sb[:], in_=wgo)
 
-        def half_of(lst, h):
-            return lst[:, 32 * h : 32 * (h + 1)]
+        lists = (src_list, dst_list)
+
+        def half_of(which, h):
+            return lists[which][:, 32 * h : 32 * (h + 1)]
 
         g_w = {}
         g_s = {}
+
+        def gather_scales(which, h):
+            g_s[which, h] = keep.tile([P, HALF], U8, name="g_s%d%d" % (which, h), align_bytes=64)
+            nc.vector.tensor_copy(out=g_s[which, h][:], in_=tab_s[:].indirect(half_of(which, h)))
+
+        def gather_words(a, h, tag):
+            both = keep.tile([P, 2, HALF], U32, name="g_w%d%d" % (a, h), tag=tag, align_bytes=64)
+            for which in (SRC, DST):
+                g_w[which, a, h] = both[:, which, :]
+                nc.vector.tensor_copy(out=g_w[which, a, h], in_=tab_w[a][:].indirect(half_of(which, h)))
+
         for h in range(2):
-            for which, lst in enumerate((src_list, dst_list)):
-                g_s[which, h] = keep.tile([P, HALF], U8, name="g_s%d%d" % (which, h), align_bytes=64)
-                nc.vector.tensor_copy(out=g_s[which, h][:], in_=tab_s[:].indirect(half_of(lst, h)))
+            for which in (SRC, DST):
+                gather_scales(which, h)
         for a in range(PASSES):
-            for h in range(2):
-                for which, lst in enumerate((src_list, dst_list)):
-                    g_w[which, a, h] = keep.tile([P, HALF], U32, name="g_w%d%d%d" % (which, a, h), align_bytes=64)
-                    nc.vector.tensor_copy(out=g_w[which, a, h][:], in_=tab_w[a][:].indirect(half_of(lst, h)))
+            gather_words(a, 0, "g_w%d0" % a)
 
-        wa_w = []
-        wa_s = []
+        wa_w = [keep.tile([P, N], U32, name="wa_w%d" % a, align_bytes=64) for a in range(PASSES)]
+        wa_s = [keep.tile([P, N], U8, name="wa_s%d" % a, align_bytes=64) for a in range(PASSES)]
         for a in range(PASSES):
-            grouped = keep.tile([P, N * PACK], BF16, name="wa_grouped%d" % a, align_bytes=64)
-            nc.scalar.copy(
-                out=grouped[:].rearrange("p (t m i) -> p m t i", t=PACK, i=PACK),
-                in_=wa_raw[a][:].rearrange("p i (m t) -> p m t i", t=PACK),
-            )
-            codes = keep.tile([P, N], U32, name="wa_w%d" % a, align_bytes=64)
-            plane = keep.tile([P, N], U8, name="wa_s%d" % a, align_bytes=64)
-            nc.vector.quantize_mx(out=codes[:].bitcast(FP8X4), scales=plane[:], in_=grouped[:])
-            wa_w.append(codes)
-            wa_s.append(plane)
+            for s in range(2):
+                grouped = keep.tile([P, N // 2 * PACK], BF16, name="wa_grouped%d%d" % (a, s), tag="grouped%d%d" % (a, s), align_bytes=64)
+                by_word = grouped[:].rearrange("p (c v i) -> p c i v", v=4, i=PACK)
+                by_row = wa_raw[a, s][:].rearrange("p i (c v) -> p c i v", v=4)
+                if (a, s) == (1, 1):
+                    nc.gpsimd.tensor_scalar(out=by_word, in0=by_row, scalar1=1.0, scalar2=0.0, op0=ALU.mult, op1=ALU.add)
+                else:
+                    nc.scalar.copy(out=by_word, in_=by_row)
+                cols = slice(N // 2 * s, N // 2 * (s + 1))
+                nc.vector.quantize_mx(out=wa_w[a][:, cols].bitcast(FP8X4), scales=wa_s[a][:, cols], in_=grouped[:])
+        gather_words(0, 1, "wa_raw11")
+        gather_words(1, 1, "grouped11")
 
-        w_dealt = []
-        for pos, raw in enumerate(w_raw):
-            per_pass = []
-            for a in range(PASSES):
-                dealt = keep.tile([P, N], U32, name="w_dealt%d%d" % (pos, a), align_bytes=64)
-                nc.scalar.copy(
-                    out=dealt[:].rearrange("p (t u v) -> p u t v", t=PACK, v=4),
-                    in_=raw[:, a, :].rearrange("p (u v t) -> p u t v", t=PACK, v=4),
-                )
-                per_pass.append(dealt)
-            w_dealt.append(per_pass)
-        wc_w, wb_w = w_dealt
-        w_s = keep.tile([P, N], U8, name="w_s", align_bytes=64)
-        nc.gpsimd.tensor_copy(
-            out=w_s[:].rearrange("p (t u v) -> p u t v", t=PACK, v=16),
-            in_=w_s_raw[:].rearrange("p (u v t) -> p u t v", t=PACK, v=16),
-        )
+        banks_taken = []
+
+        def next_bank():
+            banks_taken.append(len(banks_taken) % 8)
+            return "bank%d" % banks_taken[-1]
+
+        wgo_ps = psum.tile([P, HALF], F32, name="wgo_ps", tag=next_bank())
+        nc.tensor.transpose(wgo_ps[:, 0:P], wgo_rows[:], ident[:])
+        wgo_col = keep.tile([P, J // P], F32, name="wgo_col", align_bytes=64)
+        nc.scalar.copy(out=wgo_col[:], in_=wgo_ps[:, 0 : J // P])
 
         r_g = {}
-        for t in PAGE_ORDER:
-            for h in range(2):
-                r_g[t, h] = keep.tile([P, HALF], F32, name="r_g%d%d" % (t, h), align_bytes=64)
-                nc.vector.tensor_copy(out=r_g[t, h][:], in_=r_pages[t][:].indirect(half_of(dst_list, h)))
+        for pos, h in HALF_ORDER:
+            t = PAGE_ORDER[pos]
+            r_g[t, h] = keep.tile([P, HALF], F32, name="r_g%d%d" % (t, h), align_bytes=64)
+            nc.vector.tensor_copy(out=r_g[t, h][:], in_=r_pages[t][:].indirect(half_of(DST, h)))
 
-        def mx(acc, w, w_plane, w_row, t, which, a, h, start, stop):
-            cols = slice(P * t, P * (t + 1))
+        def mx(acc, w, w_plane, which, a, jb, start, stop):
+            h, b = divmod(jb, BLOCKS)
+            cols = slice(P * b, P * (b + 1))
             nc.tensor.matmul_mx(
                 out=acc[:],
-                lhsT=w[:, cols].bitcast(FP8X4),
-                lhsT_scale=w_plane[w_row:P, cols],
-                rhs=g_w[which, a, h][:].bitcast(FP8X4),
-                rhs_scale=g_s[which, h][8 + 4 * a : P, :],
+                lhsT=g_w[which, a, h][:, cols].bitcast(FP8X4),
+                lhsT_scale=g_s[which, h][4 * a : P, cols],
+                rhs=w.bitcast(FP8X4),
+                rhs_scale=w_plane,
                 start=start,
                 stop=stop,
             )
 
-        inter = [keep.tile([P, w, PACK], BF16, name="inter%d" % c, align_bytes=64) for c, (c0, w) in enumerate(CHUNKS)]
+        def dealt(bank):
+            return bank[:].rearrange("j (p t) -> j t p", t=PACK)
+
+        ms_sb = {}
+        ms_half = []
+        za_ps = {}
+        msg = {}
+
+        def message(jb):
+            ms_ps = psum.tile([P, N], F32, name="ms_ps", tag=next_bank())
+            for a in range(PASSES):
+                mx(ms_ps, wc_w[:, a, :], w_s[8 + 4 * a : P, :], SRC, a, jb, a == 0, a == PASSES - 1)
+            if jb % BLOCKS == 0:
+                ms_half.append(keep.tile([P, BLOCKS, PACK, P], F32, name="ms_half%d" % (jb // BLOCKS), tag=("wa_raw10", "wa_raw00")[jb // BLOCKS], align_bytes=64))
+            ms_sb[jb] = ms_half[-1][:, jb % BLOCKS, :, :]
+            nc.scalar.activation(out=ms_sb[jb], in_=dealt(ms_ps), func=ACT.Copy, scale=wgo_col[:, jb : jb + 1])
+
+        def gate_source_part(jb):
+            za_ps[jb] = psum.tile([P, N], F32, name="za_ps", tag=next_bank())
+            for a in range(PASSES):
+                mx(za_ps[jb], wb_w[:, a, :], w_s[4 * a : P, :], SRC, a, jb, a == 0, False)
+
+        def gate_target_part(jb):
+            for a in range(PASSES):
+                mx(za_ps[jb], wa_w[a][:], wa_s[a][:], DST, a, jb, False, a == PASSES - 1)
+            msg[jb] = keep.tile([P, PACK, P], F32, name="msg%d" % jb, tag="msg%d" % jb, align_bytes=64)
+            nc.scalar.activation(out=msg[jb][:], in_=dealt(za_ps[jb]), func=ACT.Sigmoid)
+            nc.gpsimd.tensor_tensor(out=msg[jb][:], in0=msg[jb][:], in1=ms_sb[jb], op=ALU.mult)
+
         out_rows = out_0.rearrange("(p t) c -> p t c", t=PACK)
-        unit = 0
-        for pos, t in enumerate(PAGE_ORDER):
-            for h in range(2):
-                ms_ps = psum.tile([P, HALF], F32, name="ms_ps")
-                for a in range(PASSES):
-                    mx(ms_ps, wc_w[a], w_s, 8 + 4 * a, t, 0, a, h, a == 0, a == PASSES - 1)
-                za_ps = psum.tile([P, HALF], F32, name="za_ps")
-                for a in range(PASSES):
-                    mx(za_ps, wb_w[a], w_s, 4 * a, t, 0, a, h, a == 0, False)
-                for a in range(PASSES):
-                    mx(za_ps, wa_w[a], wa_s[a], 0, t, 1, a, h, False, a == PASSES - 1)
-                val = ring.tile([P, HALF], F32, name="val")
-                if unit in VECTOR_PRODUCT:
-                    nc.scalar.activation(out=val[:], in_=za_ps[:], func=ACT.Sigmoid)
-                    nc.vector.tensor_tensor(out=val[:], in0=ms_ps[:], in1=val[:], op=ALU.mult)
-                else:
-                    ms_sb = ring.tile([P, HALF], F32, name="ms_sb")
-                    nc.scalar.copy(out=ms_sb[:], in_=ms_ps[:])
-                    nc.scalar.activation(out=val[:], in_=za_ps[:], func=ACT.Sigmoid)
-                    nc.gpsimd.tensor_tensor(out=val[:], in0=val[:], in1=ms_sb[:], op=ALU.mult)
-                nc.gpsimd.tensor_tensor(out=val[:], in0=val[:], in1=r_g[t, h][:], op=ALU.add)
-                nc.gpsimd.tensor_tensor(out=val[:], in0=val[:], in1=wgo_sb[:, HALF * h : HALF * (h + 1)], op=ALU.mult)
-                nc.vector.tensor_copy(out=pages[t][:].indirect(half_of(dst_list, h)), in_=val[:])
-                unit = unit + 1
-            nc.sync.dma_start(out=out_rows[:, t, :], in_=pages[t][:])
-            for c, (c0, w) in enumerate(CHUNKS):
+
+        def put_half(u):
+            pos, h = HALF_ORDER[u]
+            t = PAGE_ORDER[pos]
+            r_ps = psum.tile([P, HALF], F32, name="r_ps", tag=next_bank())
+            r_w = ring.tile([P, BLOCKS, P], F32, name="r_w", bufs=3)
+            for b in range(BLOCKS):
+                cols = slice(P * b, P * (b + 1))
+                nc.tensor.transpose(r_ps[:, cols], r_g[t, h][:, cols], ident[:])
+            for b in range(BLOCKS):
+                jb = BLOCKS * h + b
+                nc.scalar.activation(
+                    out=r_w[:, b, :], in_=r_ps[:, P * b : P * (b + 1)], func=ACT.Copy, scale=wgo_col[:, jb : jb + 1]
+                )
+            sum_ps = psum.tile([P, HALF], F32, name="sum_ps", tag=next_bank())
+            for b in range(BLOCKS):
+                cols = slice(P * b, P * (b + 1))
+                nc.tensor.matmul(
+                    sum_ps[:, cols], lhsT=msg[BLOCKS * h + b][:, t, :], rhs=ident[:],
+                    start=True, stop=False, is_transpose=True,
+                )
+                nc.tensor.matmul(
+                    sum_ps[:, cols], lhsT=r_w[:, b, :], rhs=ident[:], start=False, stop=True, is_transpose=True
+                )
+            val = ring.tile([P, HALF], F32, name="val")
+            nc.scalar.copy(out=val[:], in_=sum_ps[:])
+            nc.vector.tensor_copy(out=pages[t][:].indirect(half_of(DST, h)), in_=val[:])
+            if h == 1:
+                nc.sync.dma_start(out=out_rows[:, t, :], in_=pages[t][:])
+
+        inter = {}
+
+        def round_page(pos, chunks):
+            t = PAGE_ORDER[pos]
+            for c in chunks:
+                c0, w = CHUNKS[c]
+                if pos == 0:
+                    inter[c] = keep.tile([P, w, PACK], BF16, name="inter%d" % c, tag="msg%d" % c, align_bytes=64)
                 if pos == PACK - 1 and c < VECTOR_CHUNKS:
                     nc.vector.tensor_copy(out=inter[c][:, :, t], in_=pages[t][:, c0 : c0 + w])
+                elif t < 2 and c in GPSIMD_CHUNKS:
+                    nc.gpsimd.tensor_scalar(
+                        out=inter[c][:, :, t], in0=pages[t][:, c0 : c0 + w], scalar1=1.0, scalar2=0.0,
+                        op0=ALU.mult, op1=ALU.add,
+                    )
                 else:
                     nc.scalar.copy(out=inter[c][:, :, t], in_=pages[t][:, c0 : c0 + w])
+
+        for jb in range(2 * BLOCKS):
+            message(jb)
+            gate_source_part(jb)
+            gate_target_part(jb)
+            if jb == 5:
+                for u in range(1):
+                    put_half(u)
+        for u in range(1, 2 * PACK - 1):
+            put_half(u)
+        round_page(0, range(VECTOR_CHUNKS))
+        put_half(2 * PACK - 1)
+        round_page(0, range(VECTOR_CHUNKS, len(CHUNKS)))
+        for pos in range(1, PACK):
+            round_page(pos, range(len(CHUNKS)))
 
         out_s = keep.tile([P, T], U8, name="out_s", align_bytes=64)
         out_words = out_1[0].rearrange("p t i -> p (t i)").bitcast(I32)

@@ -53,14 +53,15 @@ def tile_list_rgg_LP_kernel(
                 wa_raw[a, s] = keep.tile([P, PACK, N // 2], F32, name="wa_raw%d%d" % (a, s), tag="wa_raw%d%d" % (a, s), align_bytes=64)
         wgo_rows = keep.tile([P, P], F32, name="wgo_rows", align_bytes=64)
         r_pages = [keep.tile([P, T], F32, name="r_page%d" % t, align_bytes=64) for t in range(PACK)]
-        pages = [keep.tile([P, T], F32, name="page%d" % t, align_bytes=64) for t in range(PACK)]
+        pages = {}
         ident = keep.tile([P, P], F32, name="ident", align_bytes=64)
 
         nc.vector.memset(tab_s[:].bitcast(I32), 0)
         nc.vector.memset(w_s[:].bitcast(I32), 0)
         make_identity(nc, ident[:])
-        for t in PAGE_ORDER:
-            nc.gpsimd.memset(pages[t][:], 0.0)
+        for t in PAGE_ORDER[:3]:
+            pages[t] = keep.tile([P, T], F32, name="page%d" % t, align_bytes=64)
+            nc.vector.memset(pages[t][:], 0.0)
 
         def load_table_words(a):
             nc.sync.dma_start(out=tab_w[a][:].bitcast(I32), in_=tab_words[a].rearrange("p t i -> p (t i)").bitcast(I32))
@@ -135,7 +136,7 @@ def tile_list_rgg_LP_kernel(
                 grouped = keep.tile([P, N // 2 * PACK], BF16, name="wa_grouped%d%d" % (a, s), tag="grouped%d%d" % (a, s), align_bytes=64)
                 by_word = grouped[:].rearrange("p (c v i) -> p c i v", v=4, i=PACK)
                 by_row = wa_raw[a, s][:].rearrange("p i (c v) -> p c i v", v=4)
-                if (a, s) == (1, 1):
+                if False:
                     nc.gpsimd.tensor_scalar(out=by_word, in0=by_row, scalar1=1.0, scalar2=0.0, op0=ALU.mult, op1=ALU.add)
                 else:
                     nc.scalar.copy(out=by_word, in_=by_row)
@@ -259,6 +260,9 @@ def tile_list_rgg_LP_kernel(
             if jb == 5:
                 for u in range(1):
                     put_half(u)
+        for t in PAGE_ORDER[3:]:
+            pages[t] = keep.tile([P, T], F32, name="page%d" % t, tag="wa_raw00", align_bytes=64)
+            nc.gpsimd.memset(pages[t][:], 0.0)
         for u in range(1, 2 * PACK - 1):
             put_half(u)
         round_page(0, range(VECTOR_CHUNKS))

@@ -18,16 +18,22 @@ ACT = mybir.ActivationFunctionType
 
 P = 128
 PACK = 4
-PASSES = 2
-HALF = 512
-BLOCKS = HALF // P
+PASSES = K // (P * PACK)
+HALF = J // 2
+TILES_PER_HALF = HALF // P
+EDGE_TILES = J // P
+WA_COLS = N // 2
+PSUM_BANKS = 8
 SRC, DST = 0, 1
+TAB_ROW, WB_ROW, WC_ROW = 0, 0, 8
+
 PAGE_ORDER = (2, 0, 1, 3)
 HALF_ORDER = ((0, 0), (1, 0), (0, 1), (1, 1), (2, 0), (2, 1), (3, 0), (3, 1))
+FIRST_PUT_AFTER = 5
 CHUNKS = ((0, 512), (512, 384), (896, 384), (1280, 384), (1664, 384))
 VECTOR_CHUNKS = 2
-GPSIMD_CHUNKS = (2, 3, 4,)
 STORE_GROUPS = ((0, 1), (2, 3), (4,))
+R_TURNED_BUFS = 3
 
 
 def tile_list_rgg_LP_kernel(
@@ -37,7 +43,7 @@ def tile_list_rgg_LP_kernel(
     nc = tc.nc
     with ExitStack() as ctx:
         keep = ctx.enter_context(tc.tile_pool(name="keep", bufs=1))
-        ring = ctx.enter_context(tc.tile_pool(name="ring", bufs=8))
+        ring = ctx.enter_context(tc.tile_pool(name="ring", bufs=len(HALF_ORDER)))
         psum = ctx.enter_context(tc.psum_pool(name="psum", bufs=1))
 
         src_list = keep.tile([P, J // 16], U16, name="src_list")
@@ -50,65 +56,61 @@ def tile_list_rgg_LP_kernel(
         wa_raw = {}
         for a in range(PASSES):
             for s in range(2):
-                wa_raw[a, s] = keep.tile([P, PACK, N // 2], F32, name="wa_raw%d%d" % (a, s), tag="wa_raw%d%d" % (a, s), align_bytes=64)
+                label = "wa_raw%d%d" % (a, s)
+                wa_raw[a, s] = keep.tile([P, PACK, WA_COLS], F32, name=label, tag=label, align_bytes=64)
         wgo_rows = keep.tile([P, P], F32, name="wgo_rows", align_bytes=64)
         r_pages = [keep.tile([P, T], F32, name="r_page%d" % t, align_bytes=64) for t in range(PACK)]
-        pages = {}
         ident = keep.tile([P, P], F32, name="ident", align_bytes=64)
 
-        nc.vector.memset(tab_s[:].bitcast(I32), 0)
-        nc.vector.memset(w_s[:].bitcast(I32), 0)
+        nc.gpsimd.memset(tab_s[:].bitcast(I32), 0)
+        nc.gpsimd.memset(w_s[:].bitcast(I32), 0)
         make_identity(nc, ident[:])
-        for t in PAGE_ORDER[:3]:
+        pages = {}
+        for t in PAGE_ORDER[:-1]:
             pages[t] = keep.tile([P, T], F32, name="page%d" % t, align_bytes=64)
-            nc.vector.memset(pages[t][:], 0.0)
+            nc.gpsimd.memset(pages[t][:], 0.0)
 
         def load_table_words(a):
             nc.sync.dma_start(out=tab_w[a][:].bitcast(I32), in_=tab_words[a].rearrange("p t i -> p (t i)").bitcast(I32))
 
-        def load_weight_words(tile, words):
-            nc.sync.dma_start(out=tile[:].bitcast(I32), in_=words.rearrange("a p n i -> p a (n i)").bitcast(I32))
+        def load_weight_words(tile, words, a):
+            nc.sync.dma_start(out=tile[:, a, :].bitcast(I32), in_=words[a].rearrange("p n i -> p (n i)").bitcast(I32))
 
         def load_scale_rows(tile, first_row, scales, q):
             nc.sync.dma_start(
-                out=tile[32 * q + first_row : 32 * q + first_row + 8, :].bitcast(I32),
+                out=tile[32 * q + first_row : 32 * q + first_row + 4 * PASSES, :].bitcast(I32),
                 in_=scales[:, 4 * q : 4 * q + 4, :].bitcast(I32),
             )
 
         def load_wa(a):
-            rows = wa[512 * a : 512 * (a + 1), :].rearrange("(p i) n -> p i n", i=PACK)
+            rows = wa[P * PACK * a : P * PACK * (a + 1), :].rearrange("(p i) n -> p i n", i=PACK)
             for s in range(2):
-                nc.sync.dma_start(out=wa_raw[a, s][:], in_=rows[:, :, N // 2 * s : N // 2 * (s + 1)])
+                nc.sync.dma_start(out=wa_raw[a, s][:], in_=rows[:, :, WA_COLS * s : WA_COLS * (s + 1)])
 
-        r_rows = rT.rearrange("(p t) c -> p t c", t=PACK)
         nc.sync.dma_start(src_list[:], offs)
-        load_weight_words(wc_w, wc_words)
-        load_scale_rows(tab_s, 0, tab_scales, 0)
-        load_scale_rows(tab_s, 0, tab_scales, 1)
-        load_scale_rows(tab_s, 0, tab_scales, 2)
-        load_scale_rows(tab_s, 0, tab_scales, 3)
+        load_weight_words(wc_w, wc_words, 0)
         nc.sync.dma_start(dst_list[:], offs2)
-        load_table_words(0)
-        load_table_words(1)
-        load_scale_rows(w_s, 8, wc_scales, 0)
-        load_scale_rows(w_s, 0, wb_scales, 0)
-        load_scale_rows(w_s, 8, wc_scales, 1)
-        load_scale_rows(w_s, 0, wb_scales, 1)
-        nc.sync.dma_start(out=wgo_rows[:], in_=wgo[0:16, :].rearrange("r (b j) -> (r b) j", j=P))
-        load_wa(0)
-        load_scale_rows(w_s, 8, wc_scales, 2)
-        load_scale_rows(w_s, 0, wb_scales, 2)
-        load_scale_rows(w_s, 8, wc_scales, 3)
-        load_scale_rows(w_s, 0, wb_scales, 3)
-        load_wa(1)
-        load_weight_words(wb_w, wb_words)
+        nc.sync.dma_start(out=wgo_rows[:], in_=wgo[0 : P // EDGE_TILES, :].rearrange("r (b j) -> (r b) j", j=P))
+        for q in range(4):
+            load_scale_rows(tab_s, TAB_ROW, tab_scales, q)
+        for a in range(PASSES):
+            load_table_words(a)
+        load_weight_words(wc_w, wc_words, 1)
+        for a in range(PASSES):
+            for q in (2 * a, 2 * a + 1):
+                load_scale_rows(w_s, WC_ROW, wc_scales, q)
+                load_scale_rows(w_s, WB_ROW, wb_scales, q)
+            load_wa(a)
+        for a in range(PASSES):
+            load_weight_words(wb_w, wb_words, a)
+        r_rows = rT.rearrange("(p t) c -> p t c", t=PACK)
         for t in PAGE_ORDER:
             nc.sync.dma_start(out=r_pages[t][:], in_=r_rows[:, t, :])
 
         lists = (src_list, dst_list)
 
         def half_of(which, h):
-            return lists[which][:, 32 * h : 32 * (h + 1)]
+            return lists[which][:, HALF // 16 * h : HALF // 16 * (h + 1)]
 
         g_w = {}
         g_s = {}
@@ -117,92 +119,96 @@ def tile_list_rgg_LP_kernel(
             g_s[which, h] = keep.tile([P, HALF], U8, name="g_s%d%d" % (which, h), align_bytes=64)
             nc.vector.tensor_copy(out=g_s[which, h][:], in_=tab_s[:].indirect(half_of(which, h)))
 
-        def gather_words(a, h, tag):
-            both = keep.tile([P, 2, HALF], U32, name="g_w%d%d" % (a, h), tag=tag, align_bytes=64)
-            for which in (SRC, DST):
-                g_w[which, a, h] = both[:, which, :]
+        def gather_words(a, h, tag, wanted):
+            label = "g_w%d%d%d" % (a, h, wanted[0])
+            picked = keep.tile([P, len(wanted), HALF], U32, name=label, tag=tag, align_bytes=64)
+            for place, which in enumerate(wanted):
+                g_w[which, a, h] = picked[:, place, :]
                 nc.vector.tensor_copy(out=g_w[which, a, h], in_=tab_w[a][:].indirect(half_of(which, h)))
 
         for h in range(2):
             for which in (SRC, DST):
                 gather_scales(which, h)
         for a in range(PASSES):
-            gather_words(a, 0, "g_w%d0" % a)
+            gather_words(a, 0, "g_w%d0" % a, (SRC, DST))
+        gather_words(0, 1, "g_w01", (SRC,))
 
         wa_w = [keep.tile([P, N], U32, name="wa_w%d" % a, align_bytes=64) for a in range(PASSES)]
         wa_s = [keep.tile([P, N], U8, name="wa_s%d" % a, align_bytes=64) for a in range(PASSES)]
         for a in range(PASSES):
             for s in range(2):
-                grouped = keep.tile([P, N // 2 * PACK], BF16, name="wa_grouped%d%d" % (a, s), tag="grouped%d%d" % (a, s), align_bytes=64)
-                by_word = grouped[:].rearrange("p (c v i) -> p c i v", v=4, i=PACK)
-                by_row = wa_raw[a, s][:].rearrange("p i (c v) -> p c i v", v=4)
-                if False:
-                    nc.gpsimd.tensor_scalar(out=by_word, in0=by_row, scalar1=1.0, scalar2=0.0, op0=ALU.mult, op1=ALU.add)
-                else:
-                    nc.scalar.copy(out=by_word, in_=by_row)
-                cols = slice(N // 2 * s, N // 2 * (s + 1))
+                label = "grouped%d%d" % (a, s)
+                grouped = keep.tile([P, WA_COLS * PACK], BF16, name=label, tag=label, align_bytes=64)
+                nc.scalar.copy(
+                    out=grouped[:].rearrange("p (c v i) -> p c i v", v=4, i=PACK),
+                    in_=wa_raw[a, s][:].rearrange("p i (c v) -> p c i v", v=4),
+                )
+                cols = slice(WA_COLS * s, WA_COLS * (s + 1))
                 nc.vector.quantize_mx(out=wa_w[a][:, cols].bitcast(FP8X4), scales=wa_s[a][:, cols], in_=grouped[:])
-        gather_words(0, 1, "wa_raw11")
-        gather_words(1, 1, "grouped11")
+        gather_words(0, 1, "wa_raw11", (DST,))
+        gather_words(1, 1, "grouped11", (SRC, DST))
 
         banks_taken = []
 
         def next_bank():
-            banks_taken.append(len(banks_taken) % 8)
+            banks_taken.append(len(banks_taken) % PSUM_BANKS)
             return "bank%d" % banks_taken[-1]
 
         wgo_ps = psum.tile([P, HALF], F32, name="wgo_ps", tag=next_bank())
         nc.tensor.transpose(wgo_ps[:, 0:P], wgo_rows[:], ident[:])
-        wgo_col = keep.tile([P, J // P], F32, name="wgo_col", align_bytes=64)
-        nc.scalar.copy(out=wgo_col[:], in_=wgo_ps[:, 0 : J // P])
+        wgo_col = keep.tile([P, EDGE_TILES], F32, name="wgo_col", align_bytes=64)
+        nc.scalar.copy(out=wgo_col[:], in_=wgo_ps[:, 0:EDGE_TILES])
 
         r_g = {}
         for pos, h in HALF_ORDER:
             t = PAGE_ORDER[pos]
-            r_g[t, h] = keep.tile([P, HALF], F32, name="r_g%d%d" % (t, h), align_bytes=64)
+            r_g[t, h] = keep.tile(
+                [P, HALF], F32, name="r_g%d%d" % (t, h), tag="r_g%d%d" % (pos, h), align_bytes=64
+            )
             nc.vector.tensor_copy(out=r_g[t, h][:], in_=r_pages[t][:].indirect(half_of(DST, h)))
 
         def mx(acc, w, w_plane, which, a, jb, start, stop):
-            h, b = divmod(jb, BLOCKS)
+            h, b = divmod(jb, TILES_PER_HALF)
             cols = slice(P * b, P * (b + 1))
             nc.tensor.matmul_mx(
                 out=acc[:],
                 lhsT=g_w[which, a, h][:, cols].bitcast(FP8X4),
-                lhsT_scale=g_s[which, h][4 * a : P, cols],
+                lhsT_scale=g_s[which, h][TAB_ROW + 4 * a : P, cols],
                 rhs=w.bitcast(FP8X4),
                 rhs_scale=w_plane,
                 start=start,
                 stop=stop,
             )
 
-        def dealt(bank):
+        def by_page(bank):
             return bank[:].rearrange("j (p t) -> j t p", t=PACK)
 
-        ms_sb = {}
+        ms_tags = ("wa_raw10", "wa_raw00")
         ms_half = []
-        za_ps = {}
         msg = {}
 
-        def message(jb):
+        def gated_message(jb):
+            h, b = divmod(jb, TILES_PER_HALF)
             ms_ps = psum.tile([P, N], F32, name="ms_ps", tag=next_bank())
             for a in range(PASSES):
-                mx(ms_ps, wc_w[:, a, :], w_s[8 + 4 * a : P, :], SRC, a, jb, a == 0, a == PASSES - 1)
-            if jb % BLOCKS == 0:
-                ms_half.append(keep.tile([P, BLOCKS, PACK, P], F32, name="ms_half%d" % (jb // BLOCKS), tag=("wa_raw10", "wa_raw00")[jb // BLOCKS], align_bytes=64))
-            ms_sb[jb] = ms_half[-1][:, jb % BLOCKS, :, :]
-            nc.scalar.activation(out=ms_sb[jb], in_=dealt(ms_ps), func=ACT.Copy, scale=wgo_col[:, jb : jb + 1])
+                mx(ms_ps, wc_w[:, a, :], w_s[WC_ROW + 4 * a : P, :], SRC, a, jb, a == 0, a == PASSES - 1)
+            if b == 0:
+                ms_half.append(
+                    keep.tile(
+                        [P, TILES_PER_HALF, PACK, P], F32, name="ms_half%d" % h, tag=ms_tags[h], align_bytes=64
+                    )
+                )
+            ms_sb = ms_half[h][:, b, :, :]
+            nc.scalar.activation(out=ms_sb, in_=by_page(ms_ps), func=ACT.Copy, scale=wgo_col[:, jb : jb + 1])
 
-        def gate_source_part(jb):
-            za_ps[jb] = psum.tile([P, N], F32, name="za_ps", tag=next_bank())
+            za_ps = psum.tile([P, N], F32, name="za_ps", tag=next_bank())
             for a in range(PASSES):
-                mx(za_ps[jb], wb_w[:, a, :], w_s[4 * a : P, :], SRC, a, jb, a == 0, False)
-
-        def gate_target_part(jb):
+                mx(za_ps, wb_w[:, a, :], w_s[WB_ROW + 4 * a : P, :], SRC, a, jb, a == 0, False)
             for a in range(PASSES):
-                mx(za_ps[jb], wa_w[a][:], wa_s[a][:], DST, a, jb, False, a == PASSES - 1)
+                mx(za_ps, wa_w[a][:], wa_s[a][:], DST, a, jb, False, a == PASSES - 1)
             msg[jb] = keep.tile([P, PACK, P], F32, name="msg%d" % jb, tag="msg%d" % jb, align_bytes=64)
-            nc.scalar.activation(out=msg[jb][:], in_=dealt(za_ps[jb]), func=ACT.Sigmoid)
-            nc.gpsimd.tensor_tensor(out=msg[jb][:], in0=msg[jb][:], in1=ms_sb[jb], op=ALU.mult)
+            nc.scalar.activation(out=msg[jb][:], in_=by_page(za_ps), func=ACT.Sigmoid)
+            nc.gpsimd.tensor_tensor(out=msg[jb][:], in0=msg[jb][:], in1=ms_sb, op=ALU.mult)
 
         out_rows = out_0.rearrange("(p t) c -> p t c", t=PACK)
 
@@ -210,24 +216,26 @@ def tile_list_rgg_LP_kernel(
             pos, h = HALF_ORDER[u]
             t = PAGE_ORDER[pos]
             r_ps = psum.tile([P, HALF], F32, name="r_ps", tag=next_bank())
-            r_w = ring.tile([P, BLOCKS, P], F32, name="r_w", bufs=3)
-            for b in range(BLOCKS):
+            r_turned = ring.tile([P, TILES_PER_HALF, P], F32, name="r_turned", bufs=R_TURNED_BUFS)
+            for b in range(TILES_PER_HALF):
                 cols = slice(P * b, P * (b + 1))
                 nc.tensor.transpose(r_ps[:, cols], r_g[t, h][:, cols], ident[:])
-            for b in range(BLOCKS):
-                jb = BLOCKS * h + b
+            for b in range(TILES_PER_HALF):
+                jb = TILES_PER_HALF * h + b
                 nc.scalar.activation(
-                    out=r_w[:, b, :], in_=r_ps[:, P * b : P * (b + 1)], func=ACT.Copy, scale=wgo_col[:, jb : jb + 1]
+                    out=r_turned[:, b, :], in_=r_ps[:, P * b : P * (b + 1)], func=ACT.Copy,
+                    scale=wgo_col[:, jb : jb + 1],
                 )
             sum_ps = psum.tile([P, HALF], F32, name="sum_ps", tag=next_bank())
-            for b in range(BLOCKS):
+            for b in range(TILES_PER_HALF):
                 cols = slice(P * b, P * (b + 1))
                 nc.tensor.matmul(
-                    sum_ps[:, cols], lhsT=msg[BLOCKS * h + b][:, t, :], rhs=ident[:],
+                    sum_ps[:, cols], lhsT=msg[TILES_PER_HALF * h + b][:, t, :], rhs=ident[:],
                     start=True, stop=False, is_transpose=True,
                 )
                 nc.tensor.matmul(
-                    sum_ps[:, cols], lhsT=r_w[:, b, :], rhs=ident[:], start=False, stop=True, is_transpose=True
+                    sum_ps[:, cols], lhsT=r_turned[:, b, :], rhs=ident[:],
+                    start=False, stop=True, is_transpose=True,
                 )
             val = ring.tile([P, HALF], F32, name="val")
             nc.scalar.copy(out=val[:], in_=sum_ps[:])
@@ -239,35 +247,36 @@ def tile_list_rgg_LP_kernel(
 
         def round_page(pos, chunks):
             t = PAGE_ORDER[pos]
+            is_last = pos == PACK - 1
             for c in chunks:
-                c0, w = CHUNKS[c]
+                c0, width = CHUNKS[c]
                 if pos == 0:
-                    inter[c] = keep.tile([P, w, PACK], BF16, name="inter%d" % c, tag="msg%d" % c, align_bytes=64)
-                if pos == PACK - 1 and c < VECTOR_CHUNKS:
-                    nc.vector.tensor_copy(out=inter[c][:, :, t], in_=pages[t][:, c0 : c0 + w])
-                elif t < 2 and c in GPSIMD_CHUNKS:
-                    nc.gpsimd.tensor_scalar(
-                        out=inter[c][:, :, t], in0=pages[t][:, c0 : c0 + w], scalar1=1.0, scalar2=0.0,
-                        op0=ALU.mult, op1=ALU.add,
-                    )
+                    tag = "msg%d" % c if c < VECTOR_CHUNKS else "inter%d" % c
+                    inter[c] = keep.tile([P, width, PACK], BF16, name="inter%d" % c, tag=tag, align_bytes=64)
+                dst, src = inter[c][:, :, t], pages[t][:, c0 : c0 + width]
+                if is_last and c < VECTOR_CHUNKS:
+                    nc.vector.tensor_copy(out=dst, in_=src)
+                elif not is_last and c >= VECTOR_CHUNKS:
+                    nc.gpsimd.tensor_scalar(out=dst, in0=src, scalar1=1.0, scalar2=0.0, op0=ALU.mult, op1=ALU.add)
                 else:
-                    nc.scalar.copy(out=inter[c][:, :, t], in_=pages[t][:, c0 : c0 + w])
+                    nc.scalar.copy(out=dst, in_=src)
 
-        for jb in range(2 * BLOCKS):
-            message(jb)
-            gate_source_part(jb)
-            gate_target_part(jb)
-            if jb == 5:
-                for u in range(1):
-                    put_half(u)
-        for t in PAGE_ORDER[3:]:
-            pages[t] = keep.tile([P, T], F32, name="page%d" % t, tag="wa_raw00", align_bytes=64)
-            nc.gpsimd.memset(pages[t][:], 0.0)
-        for u in range(1, 2 * PACK - 1):
+        for jb in range(EDGE_TILES):
+            gated_message(jb)
+            if jb == FIRST_PUT_AFTER:
+                put_half(0)
+        last_first_half, last_second_half = len(HALF_ORDER) - 2, len(HALF_ORDER) - 1
+        for u in range(1, last_first_half):
             put_half(u)
-        round_page(0, range(VECTOR_CHUNKS))
-        put_half(2 * PACK - 1)
         round_page(0, range(VECTOR_CHUNKS, len(CHUNKS)))
+        last = PAGE_ORDER[-1]
+        pages[last] = keep.tile(
+            [P, T], F32, name="page%d" % last, tag="r_g%d%d" % HALF_ORDER[last_first_half - 1], align_bytes=64
+        )
+        nc.gpsimd.memset(pages[last][:], 0.0)
+        put_half(last_first_half)
+        round_page(0, range(VECTOR_CHUNKS))
+        put_half(last_second_half)
         for pos in range(1, PACK):
             round_page(pos, range(len(CHUNKS)))
 
@@ -275,16 +284,16 @@ def tile_list_rgg_LP_kernel(
         out_words = out_1[0].rearrange("p t i -> p (t i)").bitcast(I32)
         for g, group in enumerate(STORE_GROUPS):
             g0 = CHUNKS[group[0]][0]
-            width = sum(CHUNKS[c][1] for c in group)
-            codes = keep.tile([P, width], U32, name="out_w%d" % g, align_bytes=64)
+            group_width = sum(CHUNKS[c][1] for c in group)
+            codes = keep.tile([P, group_width], U32, name="out_w%d" % g, align_bytes=64)
             for c in group:
-                c0, w = CHUNKS[c]
+                c0, width = CHUNKS[c]
                 nc.vector.quantize_mx(
-                    out=codes[:, c0 - g0 : c0 - g0 + w].bitcast(FP8X4),
-                    scales=out_s[:, c0 : c0 + w],
+                    out=codes[:, c0 - g0 : c0 - g0 + width].bitcast(FP8X4),
+                    scales=out_s[:, c0 : c0 + width],
                     in_=inter[c][:].rearrange("p c i -> p (c i)"),
                 )
-            nc.sync.dma_start(out=out_words[:, g0 : g0 + width], in_=codes[:].bitcast(I32))
+            nc.sync.dma_start(out=out_words[:, g0 : g0 + group_width], in_=codes[:].bitcast(I32))
         for q in range(4):
             nc.sync.dma_start(
                 out=out_2[0, 4 * q : 4 * q + 4, :].bitcast(I32), in_=out_s[32 * q : 32 * q + 4, :].bitcast(I32)

from contextlib import ExitStack

import concourse.mybir as mybir
from concourse.masks import make_identity

K, N, T, J = 1024, 512, 2048, 1024
FLOPS = 2 * 3 * K * N * J

F32 = mybir.dt.float32
BF16 = mybir.dt.bfloat16
I32 = mybir.dt.int32
U32 = mybir.dt.uint32
U16 = mybir.dt.uint16
U8 = mybir.dt.uint8
FP8X4 = mybir.dt.float8_e4m3fn_x4
ALU = mybir.AluOpType
ACT = mybir.ActivationFunctionType

P = 128
PACK = 4
PASSES = K // (P * PACK)
HALF = J // 2
TILES_PER_HALF = HALF // P
EDGE_TILES = J // P
WA_COLS = N // 2
PSUM_BANKS = 8
SRC, DST = 0, 1
TAB_ROW, WB_ROW, WC_ROW = 0, 0, 8

PAGE_ORDER = (2, 0, 1, 3)
HALF_ORDER = ((0, 0), (1, 0), (0, 1), (1, 1), (2, 0), (2, 1), (3, 0), (3, 1))
FIRST_PUT_AFTER = 5
CHUNKS = ((0, 512), (512, 384), (896, 384), (1280, 384), (1664, 384))
VECTOR_CHUNKS = 2
STORE_GROUPS = ((0, 1), (2, 3), (4,))
R_TURNED_BUFS = 3


def tile_list_rgg_LP_kernel(
    tc, tab_words, tab_scales, wa, wb_words, wb_scales, wc_words, wc_scales, rT, wgo, offs, offs2,
    out_0, out_1, out_2,
):
    nc = tc.nc
    with ExitStack() as ctx:
        keep = ctx.enter_context(tc.tile_pool(name="keep", bufs=1))
        ring = ctx.enter_context(tc.tile_pool(name="ring", bufs=len(HALF_ORDER)))
        psum = ctx.enter_context(tc.psum_pool(name="psum", bufs=1))

        src_list = keep.tile([P, J // 16], U16, name="src_list")
        dst_list = keep.tile([P, J // 16], U16, name="dst_list")
        tab_w = [keep.tile([P, T], U32, name="tab_w%d" % a, align_bytes=64) for a in range(PASSES)]
        tab_s = keep.tile([P, T], U8, name="tab_s", align_bytes=64)
        w_s = keep.tile([P, N], U8, name="w_s", align_bytes=64)
        wb_w = keep.tile([P, PASSES, N], U32, name="wb_w", align_bytes=64)
        wc_w = keep.tile([P, PASSES, N], U32, name="wc_w", align_bytes=64)
        wa_raw = {}
        for a in range(PASSES):
            for s in range(2):
                label = "wa_raw%d%d" % (a, s)
                wa_raw[a, s] = keep.tile([P, PACK, WA_COLS], F32, name=label, tag=label, align_bytes=64)
        wgo_rows = keep.tile([P, P], F32, name="wgo_rows", align_bytes=64)
        r_pages = [keep.tile([P, T], F32, name="r_page%d" % t, align_bytes=64) for t in range(PACK)]
        ident = keep.tile([P, P], F32, name="ident", align_bytes=64)

        nc.gpsimd.memset(tab_s[:].bitcast(I32), 0)
        nc.gpsimd.memset(w_s[:].bitcast(I32), 0)
        make_identity(nc, ident[:])
        pages = {}
        for t in PAGE_ORDER[:-1]:
            pages[t] = keep.tile([P, T], F32, name="page%d" % t, align_bytes=64)
            nc.gpsimd.memset(pages[t][:], 0.0)

        def load_table_words(a):
            nc.sync.dma_start(out=tab_w[a][:].bitcast(I32), in_=tab_words[a].rearrange("p t i -> p (t i)").bitcast(I32))

        def load_weight_words(tile, words, a):
            nc.sync.dma_start(out=tile[:, a, :].bitcast(I32), in_=words[a].rearrange("p n i -> p (n i)").bitcast(I32))

        def load_scale_rows(tile, first_row, scales, q):
            nc.sync.dma_start(
                out=tile[32 * q + first_row : 32 * q + first_row + 4 * PASSES, :].bitcast(I32),
                in_=scales[:, 4 * q : 4 * q + 4, :].bitcast(I32),
            )

        def load_wa(a):
            rows = wa[P * PACK * a : P * PACK * (a + 1), :].rearrange("(p i) n -> p i n", i=PACK)
            for s in range(2):
                nc.sync.dma_start(out=wa_raw[a, s][:], in_=rows[:, :, WA_COLS * s : WA_COLS * (s + 1)])

        nc.sync.dma_start(src_list[:], offs)
        load_weight_words(wc_w, wc_words, 0)
        nc.sync.dma_start(dst_list[:], offs2)
        nc.sync.dma_start(out=wgo_rows[:], in_=wgo[0 : P // EDGE_TILES, :].rearrange("r (b j) -> (r b) j", j=P))
        for q in range(4):
            load_scale_rows(tab_s, TAB_ROW, tab_scales, q)
        for a in range(PASSES):
            load_table_words(a)
        load_weight_words(wc_w, wc_words, 1)
        for a in range(PASSES):
            for q in (2 * a, 2 * a + 1):
                load_scale_rows(w_s, WC_ROW, wc_scales, q)
                load_scale_rows(w_s, WB_ROW, wb_scales, q)
            load_wa(a)
        for a in range(PASSES):
            load_weight_words(wb_w, wb_words, a)
        r_rows = rT.rearrange("(p t) c -> p t c", t=PACK)
        for t in PAGE_ORDER:
            nc.sync.dma_start(out=r_pages[t][:], in_=r_rows[:, t, :])

        lists = (src_list, dst_list)

        def half_of(which, h):
            return lists[which][:, HALF // 16 * h : HALF // 16 * (h + 1)]

        g_w = {}
        g_s = {}

        def gather_scales(which, h):
            g_s[which, h] = keep.tile([P, HALF], U8, name="g_s%d%d" % (which, h), align_bytes=64)
            nc.vector.tensor_copy(out=g_s[which, h][:], in_=tab_s[:].indirect(half_of(which, h)))

        def gather_words(a, h, tag, wanted):
            label = "g_w%d%d%d" % (a, h, wanted[0])
            picked = keep.tile([P, len(wanted), HALF], U32, name=label, tag=tag, align_bytes=64)
            for place, which in enumerate(wanted):
                g_w[which, a, h] = picked[:, place, :]
                nc.vector.tensor_copy(out=g_w[which, a, h], in_=tab_w[a][:].indirect(half_of(which, h)))

        for h in range(2):
            for which in (SRC, DST):
                gather_scales(which, h)
        for a in range(PASSES):
            gather_words(a, 0, "g_w%d0" % a, (SRC, DST))
        gather_words(0, 1, "g_w01", (SRC,))

        wa_w = [keep.tile([P, N], U32, name="wa_w%d" % a, align_bytes=64) for a in range(PASSES)]
        wa_s = [keep.tile([P, N], U8, name="wa_s%d" % a, align_bytes=64) for a in range(PASSES)]
        for a in range(PASSES):
            for s in range(2):
                label = "grouped%d%d" % (a, s)
                grouped = keep.tile([P, WA_COLS * PACK], BF16, name=label, tag=label, align_bytes=64)
                nc.scalar.copy(
                    out=grouped[:].rearrange("p (c v i) -> p c i v", v=4, i=PACK),
                    in_=wa_raw[a, s][:].rearrange("p i (c v) -> p c i v", v=4),
                )
                cols = slice(WA_COLS * s, WA_COLS * (s + 1))
                nc.vector.quantize_mx(out=wa_w[a][:, cols].bitcast(FP8X4), scales=wa_s[a][:, cols], in_=grouped[:])
        gather_words(0, 1, "wa_raw11", (DST,))
        gather_words(1, 1, "grouped11", (SRC, DST))

        banks_taken = []

        def next_bank():
            banks_taken.append(len(banks_taken) % PSUM_BANKS)
            return "bank%d" % banks_taken[-1]

        wgo_ps = psum.tile([P, HALF], F32, name="wgo_ps", tag=next_bank())
        nc.tensor.transpose(wgo_ps[:, 0:P], wgo_rows[:], ident[:])
        wgo_col = keep.tile([P, EDGE_TILES], F32, name="wgo_col", align_bytes=64)
        nc.scalar.copy(out=wgo_col[:], in_=wgo_ps[:, 0:EDGE_TILES])

        r_g = {}
        for pos, h in HALF_ORDER:
            t = PAGE_ORDER[pos]
            r_g[t, h] = keep.tile(
                [P, HALF], F32, name="r_g%d%d" % (t, h), tag="r_g%d%d" % (pos, h), align_bytes=64
            )
            nc.vector.tensor_copy(out=r_g[t, h][:], in_=r_pages[t][:].indirect(half_of(DST, h)))

        def mx(acc, w, w_plane, which, a, jb, start, stop):
            h, b = divmod(jb, TILES_PER_HALF)
            cols = slice(P * b, P * (b + 1))
            nc.tensor.matmul_mx(
                out=acc[:],
                lhsT=g_w[which, a, h][:, cols].bitcast(FP8X4),
                lhsT_scale=g_s[which, h][TAB_ROW + 4 * a : P, cols],
                rhs=w.bitcast(FP8X4),
                rhs_scale=w_plane,
                start=start,
                stop=stop,
            )

        def by_page(bank):
            return bank[:].rearrange("j (p t) -> j t p", t=PACK)

        ms_tags = ("wa_raw10", "wa_raw00")
        ms_half = []
        msg = {}

        def gated_message(jb):
            h, b = divmod(jb, TILES_PER_HALF)
            ms_ps = psum.tile([P, N], F32, name="ms_ps", tag=next_bank())
            for a in range(PASSES):
                mx(ms_ps, wc_w[:, a, :], w_s[WC_ROW + 4 * a : P, :], SRC, a, jb, a == 0, a == PASSES - 1)
            if b == 0:
                ms_half.append(
                    keep.tile(
                        [P, TILES_PER_HALF, PACK, P], F32, name="ms_half%d" % h, tag=ms_tags[h], align_bytes=64
                    )
                )
            ms_sb = ms_half[h][:, b, :, :]
            nc.scalar.activation(out=ms_sb, in_=by_page(ms_ps), func=ACT.Copy, scale=wgo_col[:, jb : jb + 1])

            za_ps = psum.tile([P, N], F32, name="za_ps", tag=next_bank())
            for a in range(PASSES):
                mx(za_ps, wb_w[:, a, :], w_s[WB_ROW + 4 * a : P, :], SRC, a, jb, a == 0, False)
            for a in range(PASSES):
                mx(za_ps, wa_w[a][:], wa_s[a][:], DST, a, jb, False, a == PASSES - 1)
            msg[jb] = keep.tile([P, PACK, P], F32, name="msg%d" % jb, tag="msg%d" % jb, align_bytes=64)
            nc.scalar.activation(out=msg[jb][:], in_=by_page(za_ps), func=ACT.Sigmoid)
            nc.gpsimd.tensor_tensor(out=msg[jb][:], in0=msg[jb][:], in1=ms_sb, op=ALU.mult)

        out_rows = out_0.rearrange("(p t) c -> p t c", t=PACK)

        def put_half(u):
            pos, h = HALF_ORDER[u]
            t = PAGE_ORDER[pos]
            r_ps = psum.tile([P, HALF], F32, name="r_ps", tag=next_bank())
            r_turned = ring.tile([P, TILES_PER_HALF, P], F32, name="r_turned", bufs=R_TURNED_BUFS)
            for b in range(TILES_PER_HALF):
                cols = slice(P * b, P * (b + 1))
                nc.tensor.transpose(r_ps[:, cols], r_g[t, h][:, cols], ident[:])
            for b in range(TILES_PER_HALF):
                jb = TILES_PER_HALF * h + b
                nc.scalar.activation(
                    out=r_turned[:, b, :], in_=r_ps[:, P * b : P * (b + 1)], func=ACT.Copy,
                    scale=wgo_col[:, jb : jb + 1],
                )
            sum_ps = psum.tile([P, HALF], F32, name="sum_ps", tag=next_bank())
            for b in range(TILES_PER_HALF):
                cols = slice(P * b, P * (b + 1))
                nc.tensor.matmul(
                    sum_ps[:, cols], lhsT=msg[TILES_PER_HALF * h + b][:, t, :], rhs=ident[:],
                    start=True, stop=False, is_transpose=True,
                )
                nc.tensor.matmul(
                    sum_ps[:, cols], lhsT=r_turned[:, b, :], rhs=ident[:],
                    start=False, stop=True, is_transpose=True,
                )
            val = ring.tile([P, HALF], F32, name="val")
            nc.scalar.copy(out=val[:], in_=sum_ps[:])
            nc.vector.tensor_copy(out=pages[t][:].indirect(half_of(DST, h)), in_=val[:])
            if h == 1:
                nc.sync.dma_start(out=out_rows[:, t, :], in_=pages[t][:])

        inter = {}

        def round_page(pos, chunks):
            t = PAGE_ORDER[pos]
            is_last = pos == PACK - 1
            for c in chunks:
                c0, width = CHUNKS[c]
                if pos == 0:
                    tag = "msg%d" % c if c < VECTOR_CHUNKS else "inter%d" % c
                    inter[c] = keep.tile([P, width, PACK], BF16, name="inter%d" % c, tag=tag, align_bytes=64)
                dst, src = inter[c][:, :, t], pages[t][:, c0 : c0 + width]
                if is_last and c < VECTOR_CHUNKS:
                    nc.vector.tensor_copy(out=dst, in_=src)
                elif not is_last and c >= VECTOR_CHUNKS:
                    nc.gpsimd.tensor_scalar(out=dst, in0=src, scalar1=1.0, scalar2=0.0, op0=ALU.mult, op1=ALU.add)
                else:
                    nc.scalar.copy(out=dst, in_=src)

        for jb in range(EDGE_TILES):
            gated_message(jb)
            if jb == FIRST_PUT_AFTER:
                put_half(0)
        last_first_half, last_second_half = len(HALF_ORDER) - 2, len(HALF_ORDER) - 1
        for u in range(1, last_first_half):
            put_half(u)
        round_page(0, range(VECTOR_CHUNKS, len(CHUNKS)))
        last = PAGE_ORDER[-1]
        pages[last] = keep.tile(
            [P, T], F32, name="page%d" % last, tag="r_g%d%d" % HALF_ORDER[last_first_half - 1], align_bytes=64
        )
        nc.gpsimd.memset(pages[last][:], 0.0)
        put_half(last_first_half)
        round_page(0, range(VECTOR_CHUNKS))
        put_half(last_second_half)
        for pos in range(1, PACK):
            round_page(pos, range(len(CHUNKS)))

        out_s = keep.tile([P, T], U8, name="out_s", align_bytes=64)
        out_words = out_1[0].rearrange("p t i -> p (t i)").bitcast(I32)
        for g, group in enumerate(STORE_GROUPS):
            g0 = CHUNKS[group[0]][0]
            group_width = sum(CHUNKS[c][1] for c in group)
            codes = keep.tile([P, group_width], U32, name="out_w%d" % g, align_bytes=64)
            for c in group:
                c0, width = CHUNKS[c]
                nc.vector.quantize_mx(
                    out=codes[:, c0 - g0 : c0 - g0 + width].bitcast(FP8X4),
                    scales=out_s[:, c0 : c0 + width],
                    in_=inter[c][:].rearrange("p c i -> p (c i)"),
                )
            nc.sync.dma_start(out=out_words[:, g0 : g0 + group_width], in_=codes[:].bitcast(I32))
        for q in range(4):
            nc.sync.dma_start(
                out=out_2[0, 4 * q : 4 * q + 4, :].bitcast(I32), in_=out_s[32 * q : 32 * q + 4, :].bitcast(I32)
            )
